import numpy as np
import ml_dtypes


def mxq(x, axis, fmt="e4m3"):
    dtype, down = {"e4m3": (ml_dtypes.float8_e4m3fn, 7), "e5m2": (ml_dtypes.float8_e5m2, 14)}[fmt]
    v = np.moveaxis(np.asarray(x, np.float32).astype(ml_dtypes.bfloat16).astype(np.float64), axis, -1)
    blocks = v.reshape(v.shape[:-1] + (-1, 32))
    amax = np.abs(blocks).max(-1, keepdims=True)
    byte = np.maximum(np.where(amax > 0, np.frexp(amax)[1] - 1 + 127, 0) - down, 1)
    scale = np.exp2(byte - 127.0)
    codes = (blocks / scale).astype(np.float32).astype(dtype).astype(np.float64)
    return np.moveaxis((codes * scale).reshape(v.shape), -1, axis)


WIDE = False


def mx_kscale(k):
    if not WIDE:
        return np.ones(k)
    levels = np.array([10, -10, 5, -5, 0])
    if k % 512:
        return np.exp2(np.random.permutation(np.resize(levels, k // 32))).repeat(32)
    a = np.empty((k // 512, 16))
    for p in range(k // 512):
        a[p, :8] = np.random.permutation(np.resize(levels, 8))
        for g in range(8):
            far = levels[np.abs(levels - a[p, g]) >= 10]
            a[p, g + 8] = far[np.random.randint(len(far))]
    return np.exp2(a.ravel()).repeat(32)


def f64(x):
    return np.asarray(x).astype(np.float64)


def striped(idx):
    return np.tile(np.asarray(idx).reshape(-1, 16).T, (8, 1)).astype(np.uint16)


def unstriped(offs):
    return offs[:16].T.reshape(-1).astype(np.int64)


E2M1 = np.array([0.0, 0.5, 1.0, 1.5, 2.0, 3.0, 4.0, 6.0, -0.0, -0.5, -1.0, -1.5, -2.0, -3.0, -4.0, -6.0])


def pack_weight(w, fmt):
    k, n = w.shape
    w = f64(np.asarray(w, np.float32).astype(ml_dtypes.bfloat16)).reshape(k // 32, 32, n)
    amax = np.abs(w).max(1)
    if fmt == "e4m3":
        byte = np.frexp(amax)[1] - 1 + 127 - 7
    else:
        mant, ex = np.frexp(amax / 6.0)
        byte = np.where(mant > 0.5, ex, ex - 1) + 127
    byte = np.clip(np.where(amax > 0, byte, 1), 1, 254)
    scaled = (w * np.exp2(127.0 - byte)[:, None, :]).reshape(k, n).astype(np.float32)
    by_word = np.ascontiguousarray(scaled.reshape(k // 512, 128, 4, n).transpose(0, 1, 3, 2))
    if fmt == "e4m3":
        words = by_word.astype(ml_dtypes.float8_e4m3fn).view(np.uint8)
    else:
        c = by_word.astype(ml_dtypes.float4_e2m1fn).view(np.uint8) & 0xF
        words = (c[..., 0::2] | (c[..., 1::2] << 4)).reshape(k // 512, 128, 2 * n)
    return np.ascontiguousarray(words), np.ascontiguousarray(byte.astype(np.uint8).reshape(k // 512, 16, n))


def unpack_weight(words, scales, fmt):
    g, _, n = scales.shape
    words = np.ascontiguousarray(words).reshape(g, 128, n, -1)
    if fmt == "e4m3":
        vals = words.view(ml_dtypes.float8_e4m3fn).astype(np.float64)
    else:
        nib = np.empty((g, 128, n, 4), np.uint8)
        nib[..., 0::2] = words & 0xF
        nib[..., 1::2] = words >> 4
        vals = E2M1[nib]
    vals = vals * np.repeat(np.exp2(scales.astype(np.float64) - 127.0), 8, axis=1)[..., None]
    return vals.transpose(0, 1, 3, 2).reshape(g * 512, n)


def sigmoid(v):
    return 1.0 / (1.0 + np.exp(-v))


D, K, R, T, I, Q, G = 512, 512, 512, 2048, 512, 128, 32


def setup_inputs():
    n = np.random.standard_normal
    idx = np.random.permutation(T)[:I]
    fd = mx_kscale(D)
    fk = mx_kscale(K)
    fr = mx_kscale(R)
    keysp = pack_weight(n((D, T)) / fd[:, None], "e4m3")
    tabp = pack_weight(n((K, T)) / fk[:, None], "e4m3")
    return {
        "query": (n((D, Q)) * 0.6 / np.sqrt(D) * fd[:, None]).astype(np.float32),
        "query2": (n((D, Q)) * 1.0 / np.sqrt(D) * fd[:, None]).astype(np.float32),
        "keys_words": keysp[0],
        "keys_scales": keysp[1],
        "tab_words": tabp[0],
        "tab_scales": tabp[1],
        "w1": (n((K, R)) * 1 / np.sqrt(K) * fk[:, None]).astype(np.float32),
        "share": (np.random.uniform(0.4, 1.0, (R, 1))).astype(np.float32),
        "gout": (n((R, Q)) * 1 / np.sqrt(R) * fr[:, None]).astype(np.float32),
        "hsc": (np.random.uniform(0.7, 1.4, (R, 1)) / fr[:, None]).astype(np.float32),
        "old": (0.5 * n((Q, T))).astype(np.float32),
        "offs": striped(idx),
    }


def reference(query, query2, keys_words, keys_scales, tab_words, tab_scales, w1, share, gout, hsc, old, offs):
    idx = unstriped(offs)
    keysu = unpack_weight(keys_words, keys_scales, "e4m3")
    tabu = unpack_weight(tab_words, tab_scales, "e4m3")
    queryq = mxq(f64(query), 0, "e4m3")
    keysidxg = keysu[:, idx]
    a = queryq.T @ keysidxg
    query2q = mxq(f64(query2), 0, "e4m3")
    b = query2q.T @ keysidxg
    p = np.exp(a - np.max(a, axis=1, keepdims=True)) * sigmoid(b)
    z = np.sum(p, axis=1, keepdims=True)
    w1q = mxq(f64(w1), 0, "e4m3")
    tabidxg = tabu[:, idx]
    zh = w1q.T @ tabidxg
    mz = zh.reshape(R, G, I // G).mean(axis=2)
    mzr = np.repeat(mz, I // G, axis=1)
    hv = np.tanh(zh - mzr * f64(share))
    hs1 = hv * f64(hsc)
    goutq = mxq(f64(gout), 0, "e4m3")
    hs1q = mxq(hs1, 0, "e4m3")
    c0 = goutq.T @ hs1q
    dz = np.sum(c0 * p / np.square(z) * (-1.0), axis=1, keepdims=True)
    dp = c0 / z + dz
    da = dp * sigmoid(b) * np.exp(a - np.max(a, axis=1, keepdims=True))
    gs = da * 512.0
    gf = np.zeros((Q, T))
    gf[:, idx] = gs
    y = f64(old) + gf
    return y

@@ -1,0 +1,263 @@
+from contextlib import ExitStack
+
+import concourse.mybir as mybir
+
+D, K, R, T, I, Q, G = 512, 512, 512, 2048, 512, 128, 32
+FLOPS = 2 * (2 * D * Q * I + K * R * I + R * Q * I)
+
+F32 = mybir.dt.float32
+BF16 = mybir.dt.bfloat16
+I32 = mybir.dt.int32
+U32 = mybir.dt.uint32
+U16 = mybir.dt.uint16
+U8 = mybir.dt.uint8
+FP8X4 = mybir.dt.float8_e4m3fn_x4
+ALU = mybir.AluOpType
+ACT = mybir.ActivationFunctionType
+AXIS_X = mybir.AxisListType.X
+
+P = 128
+PACK = 4
+PAGE = I // G
+CHUNK = 128
+CHUNKS = I // CHUNK
+PAGES = CHUNK // PAGE
+KEY_ROW = 4
+STORE = 512
+
+
+def tile_attend_blrcentred_asked_kernel(
+    tc, query, query2, keys_words, keys_scales, tab_words, tab_scales, w1, share, gout, hsc, old, offs, out
+):
+    nc = tc.nc
+    with ExitStack() as ctx:
+        sb = ctx.enter_context(tc.tile_pool(name="sb", bufs=1))
+        ps = ctx.enter_context(tc.psum_pool(name="ps", bufs=1))
+
+        def tile(name, shape, dtype, tag=None):
+            return sb.tile(shape, dtype, name=name, tag=tag or name, align_bytes=64)
+
+        offsets = sb.tile([P, I // 16], U16, name="offsets")
+        tab_w = tile("tab_w", [P, T], U32)
+        tab_s = tile("tab_s", [P, T], U8)
+        key_s = tile("key_s", [P, T], U8)
+        w_raw = tile("w_raw", [P, PACK, R], F32)
+        share_sb = tile("share_sb", [P, PACK], F32)
+        hsc_sb = tile("hsc_sb", [P, PACK], F32)
+        placed = tile("placed", [P, T], F32)
+
+        def load_scale_rows(queues, plane, scales, first_row):
+            for r in range(4):
+                queues[r].dma_start(
+                    out=plane[first_row + r : P : 32, :].bitcast(I32),
+                    in_=scales[0, r:16:4, :].bitcast(I32),
+                )
+
+        def load_words(words_sb, words):
+            nc.sync.dma_start(
+                out=words_sb[:].bitcast(I32), in_=words[0].rearrange("p n t -> p (n t)").bitcast(I32)
+            )
+
+        def rows4(ap):
+            return ap.rearrange("(p j) c -> p j c", j=PACK)
+
+        nc.vector.memset(tab_s[:].bitcast(I32), 0)
+        nc.gpsimd.memset(key_s[:].bitcast(I32), 0)
+        nc.sync.dma_start(offsets[:], offs)
+        load_scale_rows([nc.scalar] * 4, tab_s, tab_scales, 0)
+        nc.sync.dma_start(out=w_raw[:], in_=rows4(w1))
+        load_words(tab_w, tab_words)
+        load_scale_rows([nc.scalar, nc.scalar, nc.gpsimd, nc.gpsimd], key_s, keys_scales, KEY_ROW)
+        nc.gpsimd.dma_start(out=share_sb[:], in_=share.rearrange("(p j) o -> p (j o)", j=PACK))
+        nc.gpsimd.dma_start(out=hsc_sb[:], in_=hsc.rearrange("(p j) o -> p (j o)", j=PACK))
+        nc.vector.memset(placed[:], 0.0)
+
+        tab_gs = tile("tab_gs", [P, I], U8)
+        tab_gw = tile("tab_gw", [P, I], U32)
+        key_gs = tile("key_gs", [P, I], U8)
+        key_gw = tile("key_gw", [P, I], U32)
+        nc.vector.tensor_copy(tab_gs[:], tab_s[:].indirect(offsets[:]))
+        key_w = tile("key_w", [P, T], U32, tag="tab_s")
+        load_words(key_w, keys_words)
+
+        w_bf = [tile("w_bf%d" % h, [P, 2 * P * PACK], BF16) for h in range(2)]
+        w_code = [tile("w_code%d" % h, [P, 2 * P], U32) for h in range(2)]
+        w_scale = [tile("w_scale%d" % h, [P, 2 * P], U8) for h in range(2)]
+        w_src = w_raw[:].rearrange("p j (m t) -> p m j t", t=PACK)
+
+        def w_dst(h):
+            return w_bf[h][:].rearrange("p (t m j) -> p m j t", t=2, j=PACK)
+
+        nc.vector.tensor_copy(out=w_dst(0), in_=w_src[:, :, :, 0:2])
+        nc.scalar.activation(out=w_dst(1), in_=w_src[:, :, :, 2:4], func=ACT.Copy)
+        q_raw = tile("q_raw", [P, 2, PACK, Q], F32, tag="w_raw")
+        nc.sync.dma_start(out=q_raw[:, 0], in_=rows4(query))
+        nc.sync.dma_start(out=q_raw[:, 1], in_=rows4(query2))
+        for h in range(2):
+            nc.vector.quantize_mx(out=w_code[h][:].bitcast(FP8X4), scales=w_scale[h][:], in_=w_bf[h][:])
+
+        g_raw = tile("g_raw", [P, PACK, Q], F32, tag="w_bf0")
+        nc.sync.dma_start(out=g_raw[:], in_=rows4(gout))
+        nshare = tile("nshare", [P, PACK], F32)
+        nc.scalar.mul(nshare[:], share_sb[:], -1.0 / PAGE)
+
+        first = CHUNK // 16
+        nc.vector.tensor_copy(tab_gw[:, :CHUNK], tab_w[:].indirect(offsets[:, :first]))
+        nc.vector.tensor_copy(tab_gw[:, CHUNK:], tab_w[:].indirect(offsets[:, first:]))
+
+        nc.vector.tensor_copy(key_gs[:], key_s[:].indirect(offsets[:]))
+        acc = tile("acc", [P, T], F32, tag="tab_w")
+        nc.sync.dma_start(out=acc[:], in_=old)
+
+        zh = [ps.tile([P, PACK, CHUNK], F32, name="zh%d" % c) for c in range(CHUNKS)]
+        for c in range(CHUNKS):
+            cols = slice(c * CHUNK, (c + 1) * CHUNK)
+            for t in range(PACK):
+                wcols = slice((t % 2) * P, (t % 2 + 1) * P)
+                nc.tensor.matmul_mx(
+                    out=zh[c][:, t, :],
+                    lhsT=w_code[t // 2][:, wcols].bitcast(FP8X4),
+                    lhsT_scale=w_scale[t // 2][:, wcols],
+                    rhs=tab_gw[:, cols].bitcast(FP8X4),
+                    rhs_scale=tab_gs[:, cols],
+                    start=True,
+                    stop=True,
+                )
+
+        def interleave(dst, src):
+            nc.scalar.copy(
+                out=dst.rearrange("p (c i j) -> p c j i", i=4, j=PACK),
+                in_=src.rearrange("p j (c i) -> p c j i", i=4),
+            )
+
+        sums = [tile("sums%d" % c, [P, PACK, PAGES], F32) for c in range(CHUNKS)]
+        shift = [tile("shift%d" % c, [P, PAGES, PACK], F32) for c in range(CHUNKS)]
+        centred = [tile("centred%d" % c, [P, CHUNK * PACK], F32) for c in range(CHUNKS)]
+        hv = [tile("hv%d" % c, [P, CHUNK * PACK], F32) for c in range(CHUNKS)]
+        h_bf = [tile("h_bf%d" % c, [P, CHUNK * PACK], BF16) for c in range(CHUNKS)]
+        h_code = [tile("h_code%d" % c, [P, CHUNK], U32) for c in range(CHUNKS)]
+        h_scale = [tile("h_scale%d" % c, [P, CHUNK], U8) for c in range(CHUNKS)]
+        c0 = ps.tile([P, I], F32, name="c0")
+
+        def page_sums(c):
+            nc.vector.tensor_reduce(
+                out=sums[c][:].rearrange("p t g -> p (t g)"),
+                in_=zh[c][:].rearrange("p t (g e) -> p (t g) e", e=PAGE),
+                axis=AXIS_X,
+                op=ALU.add,
+            )
+
+        def page_shift(c):
+            nc.vector.tensor_tensor(
+                out=shift[c][:].rearrange("p g t -> p t g"),
+                in0=sums[c][:],
+                in1=nshare[:].unsqueeze(2).broadcast_to([P, PACK, PAGES]),
+                op=ALU.mult,
+            )
+
+        def centre(c):
+            nc.vector.tensor_tensor(
+                out=centred[c][:].rearrange("p (g e t) -> p g e t", e=PAGE, t=PACK),
+                in0=zh[c][:].rearrange("p t (g e) -> p g e t", e=PAGE),
+                in1=shift[c][:].unsqueeze(2).broadcast_to([P, PAGES, PAGE, PACK]),
+                op=ALU.add,
+            )
+            nc.scalar.activation(out=hv[c][:], in_=centred[c][:], func=ACT.Tanh)
+
+        def scale_hidden(c):
+            nc.vector.tensor_tensor(
+                out=h_bf[c][:].rearrange("p (i t) -> p i t", t=PACK),
+                in0=hv[c][:].rearrange("p (i t) -> p i t", t=PACK),
+                in1=hsc_sb[:].unsqueeze(1).broadcast_to([P, CHUNK, PACK]),
+                op=ALU.mult,
+            )
+
+        g_bf = tile("g_bf", [P, Q * PACK], BF16)
+        g_code = tile("g_code", [P, Q], U32)
+        g_scale = tile("g_scale", [P, Q], U8)
+
+        def read_back(c):
+            nc.vector.quantize_mx(out=h_code[c][:].bitcast(FP8X4), scales=h_scale[c][:], in_=h_bf[c][:])
+            nc.tensor.matmul_mx(
+                out=c0[:, c * CHUNK : (c + 1) * CHUNK],
+                lhsT=g_code[:].bitcast(FP8X4),
+                lhsT_scale=g_scale[:],
+                rhs=h_code[c][:].bitcast(FP8X4),
+                rhs_scale=h_scale[c][:],
+                start=True,
+                stop=True,
+            )
+
+        q_bf = tile("q_bf", [P, 2 * Q * PACK], BF16)
+        q_code = tile("q_code", [P, 2 * Q], U32)
+        q_scale = tile("q_scale", [P, 2 * Q], U8)
+        score = [ps.tile([P, I], F32, name="score%d" % n) for n in range(2)]
+        neg_max = tile("neg_max", [P, 1], F32)
+        expo = tile("expo", [P, I], F32)
+        gate = tile("gate", [P, I], F32)
+        prob = tile("prob", [P, I], F32)
+        z = tile("z", [P, 1], F32)
+        inv_z = tile("inv_z", [P, 1], F32)
+        up = tile("up", [P, 1], F32)
+        down = tile("down", [P, 1], F32)
+        nc.vector.tensor_copy(key_gw[:], key_w[:].indirect(offsets[:]))
+        interleave(q_bf[:, : Q * PACK], q_raw[:, 0])
+        interleave(q_bf[:, Q * PACK :], q_raw[:, 1])
+        nc.vector.quantize_mx(out=q_code[:].bitcast(FP8X4), scales=q_scale[:], in_=q_bf[:])
+        for n in range(2):
+            qcols = slice(n * Q, (n + 1) * Q)
+            nc.tensor.matmul_mx(
+                out=score[n][:],
+                lhsT=q_code[:, qcols].bitcast(FP8X4),
+                lhsT_scale=q_scale[:, qcols],
+                rhs=key_gw[:].bitcast(FP8X4),
+                rhs_scale=key_gs[KEY_ROW:, :],
+                start=True,
+                stop=True,
+            )
+        nc.vector.tensor_reduce(out=neg_max[:], in_=score[0][:], axis=AXIS_X, op=ALU.max, negate=True)
+        nc.scalar.activation(out=expo[:], in_=score[0][:], func=ACT.Exp, bias=neg_max[:])
+        nc.scalar.activation(out=gate[:], in_=score[1][:], func=ACT.Sigmoid)
+        interleave(g_bf[:], g_raw[:])
+        page_sums(0)
+        page_sums(1)
+        page_shift(0)
+        page_shift(1)
+        centre(0)
+        centre(1)
+        page_sums(2)
+        page_sums(3)
+        page_shift(2)
+        page_shift(3)
+        centre(2)
+        scale_hidden(0)
+        centre(3)
+        nc.vector.quantize_mx(out=g_code[:].bitcast(FP8X4), scales=g_scale[:], in_=g_bf[:])
+        scale_hidden(1)
+        read_back(0)
+        nc.vector.scalar_tensor_tensor(
+            out=prob[:], in0=expo[:], scalar=1.0, in1=gate[:], op0=ALU.mult, op1=ALU.mult, accum_out=z[:]
+        )
+        scale_hidden(2)
+        read_back(1)
+        nc.vector.reciprocal(inv_z[:], z[:])
+        nc.scalar.mul(up[:], inv_z[:], 512.0)
+        nc.scalar.mul(down[:], inv_z[:], -1.0)
+        scale_hidden(3)
+        read_back(2)
+        read_back(3)
+
+        direct = tile("direct", [P, I], F32)
+        total = tile("total", [P, 1], F32)
+        through_z = tile("through_z", [P, I], F32)
+        nc.vector.scalar_tensor_tensor(
+            out=direct[:], in0=c0[:], scalar=up[:], in1=prob[:], op0=ALU.mult, op1=ALU.mult, accum_out=total[:]
+        )
+        nc.vector.tensor_scalar(
+            out=through_z[:], in0=prob[:], scalar1=total[:], scalar2=down[:], op0=ALU.mult, op1=ALU.mult
+        )
+        nc.vector.tensor_tensor(placed[:].indirect(offsets[:]), direct[:], through_z[:], ALU.add)
+        for s in range(T // STORE):
+            cols = slice(s * STORE, (s + 1) * STORE)
+            nc.vector.tensor_tensor(out=acc[:, cols], in0=acc[:, cols], in1=placed[:, cols], op=ALU.add)
+            nc.sync.dma_start(out=out[:, cols], in_=acc[:, cols])

@@ -38,48 +38,99 @@ def tile_attend_blrcentred_asked_kernel(
             return sb.tile(shape, dtype, name=name, tag=tag or name, align_bytes=64)
 
         offsets = sb.tile([P, I // 16], U16, name="offsets")
-        tab_w = tile("tab_w", [P, T], U32)
-        tab_s = tile("tab_s", [P, T], U8)
+        key_w = tile("key_w", [P, T], U32)
         key_s = tile("key_s", [P, T], U8)
-        w_raw = tile("w_raw", [P, PACK, R], F32)
+        q_raw = [tile("q_raw%d" % n, [P, PACK, Q], F32) for n in range(2)]
         share_sb = tile("share_sb", [P, PACK], F32)
         hsc_sb = tile("hsc_sb", [P, PACK], F32)
         placed = tile("placed", [P, T], F32)
 
-        def load_scale_rows(queues, plane, scales, first_row):
+        def load_scale_rows(queue, plane, scales, first_row):
             for r in range(4):
-                queues[r].dma_start(
+                queue.dma_start(
                     out=plane[first_row + r : P : 32, :].bitcast(I32),
                     in_=scales[0, r:16:4, :].bitcast(I32),
                 )
 
-        def load_words(words_sb, words):
-            nc.sync.dma_start(
+        def load_words(queue, words_sb, words):
+            queue.dma_start(
                 out=words_sb[:].bitcast(I32), in_=words[0].rearrange("p n t -> p (n t)").bitcast(I32)
             )
 
         def rows4(ap):
             return ap.rearrange("(p j) c -> p j c", j=PACK)
 
-        nc.vector.memset(tab_s[:].bitcast(I32), 0)
-        nc.gpsimd.memset(key_s[:].bitcast(I32), 0)
+        def interleave(copy, dst, src):
+            copy(
+                out=dst.rearrange("p (c i j) -> p c j i", i=4, j=PACK),
+                in_=src.rearrange("p j (c i) -> p c j i", i=4),
+            )
+
+        nc.vector.memset(key_s[:].bitcast(I32), 0)
         nc.sync.dma_start(offsets[:], offs)
-        load_scale_rows([nc.scalar] * 4, tab_s, tab_scales, 0)
-        nc.sync.dma_start(out=w_raw[:], in_=rows4(w1))
-        load_words(tab_w, tab_words)
-        load_scale_rows([nc.scalar, nc.scalar, nc.gpsimd, nc.gpsimd], key_s, keys_scales, KEY_ROW)
+        nc.sync.dma_start(out=q_raw[0][:], in_=rows4(query))
+        nc.sync.dma_start(out=q_raw[1][:], in_=rows4(query2))
+        load_words(nc.sync, key_w, keys_words)
+        load_scale_rows(nc.scalar, key_s, keys_scales, KEY_ROW)
         nc.gpsimd.dma_start(out=share_sb[:], in_=share.rearrange("(p j) o -> p (j o)", j=PACK))
         nc.gpsimd.dma_start(out=hsc_sb[:], in_=hsc.rearrange("(p j) o -> p (j o)", j=PACK))
         nc.vector.memset(placed[:], 0.0)
+        factors = tile("factors", [P, 2], F32)
+        nc.vector.memset(factors[:, 0:1], 512.0)
+        nc.vector.memset(factors[:, 1:2], -1.0)
+        nshare = tile("nshare", [P, PACK], F32)
+        nc.gpsimd.tensor_scalar(
+            out=nshare[:], in0=share_sb[:], scalar1=-1.0 / PAGE, scalar2=0.0, op0=ALU.mult, op1=ALU.add
+        )
 
         tab_gs = tile("tab_gs", [P, I], U8)
         tab_gw = tile("tab_gw", [P, I], U32)
         key_gs = tile("key_gs", [P, I], U8)
         key_gw = tile("key_gw", [P, I], U32)
-        nc.vector.tensor_copy(tab_gs[:], tab_s[:].indirect(offsets[:]))
-        key_w = tile("key_w", [P, T], U32, tag="tab_s")
-        load_words(key_w, keys_words)
+        q_bf = tile("q_bf", [P, 2 * Q * PACK], BF16)
+        q_code = tile("q_code", [P, 2 * Q], U32)
+        q_scale = tile("q_scale", [P, 2 * Q], U8)
+        neg_max = tile("neg_max", [P, 1], F32)
+        z = tile("z", [P, 1], F32)
+        inv_z = tile("inv_z", [P, 1], F32)
+        over_z = tile("over_z", [P, 2], F32)
 
+        interleave(nc.vector.tensor_copy, q_bf[:, : Q * PACK], q_raw[0][:])
+        w_raw = tile("w_raw", [P, PACK, R], F32, tag="q_raw0")
+        nc.sync.dma_start(out=w_raw[:], in_=rows4(w1))
+        interleave(nc.vector.tensor_copy, q_bf[:, Q * PACK :], q_raw[1][:])
+        tab_s = tile("tab_s", [P, T], U8, tag="q_raw1")
+        nc.vector.memset(tab_s[:].bitcast(I32), 0)
+        load_scale_rows(nc.scalar, tab_s, tab_scales, 0)
+        nc.vector.quantize_mx(out=q_code[:].bitcast(FP8X4), scales=q_scale[:], in_=q_bf[:])
+        tab_w = tile("tab_w", [P, T], U32, tag="q_bf")
+        load_words(nc.sync, tab_w, tab_words)
+        nc.vector.tensor_copy(key_gs[:], key_s[:].indirect(offsets[:]))
+        g_raw = tile("g_raw", [P, PACK, Q], F32, tag="key_s")
+        nc.sync.dma_start(out=g_raw[:], in_=rows4(gout))
+        nc.vector.tensor_copy(key_gw[:], key_w[:].indirect(offsets[:]))
+        acc = tile("acc", [P, T], F32, tag="key_w")
+        nc.sync.dma_start(out=acc[:], in_=old)
+
+        def scores(n):
+            bank = ps.tile([P, I], F32, name="score%d" % n)
+            qcols = slice(n * Q, (n + 1) * Q)
+            nc.tensor.matmul_mx(
+                out=bank[:],
+                lhsT=q_code[:, qcols].bitcast(FP8X4),
+                lhsT_scale=q_scale[:, qcols],
+                rhs=key_gw[:].bitcast(FP8X4),
+                rhs_scale=key_gs[KEY_ROW:, :],
+                start=True,
+                stop=True,
+            )
+            return bank
+
+        a = scores(0)
+        b = scores(1)
+        nc.vector.tensor_reduce(out=neg_max[:], in_=a[:], axis=AXIS_X, op=ALU.max, negate=True)
+
+        nc.vector.tensor_copy(tab_gs[:], tab_s[:].indirect(offsets[:]))
         w_bf = [tile("w_bf%d" % h, [P, 2 * P * PACK], BF16) for h in range(2)]
         w_code = [tile("w_code%d" % h, [P, 2 * P], U32) for h in range(2)]
         w_scale = [tile("w_scale%d" % h, [P, 2 * P], U8) for h in range(2)]
@@ -88,26 +139,18 @@ def tile_attend_blrcentred_asked_kernel(
         def w_dst(h):
             return w_bf[h][:].rearrange("p (t m j) -> p m j t", t=2, j=PACK)
 
-        nc.vector.tensor_copy(out=w_dst(0), in_=w_src[:, :, :, 0:2])
-        nc.scalar.activation(out=w_dst(1), in_=w_src[:, :, :, 2:4], func=ACT.Copy)
-        q_raw = tile("q_raw", [P, 2, PACK, Q], F32, tag="w_raw")
-        nc.sync.dma_start(out=q_raw[:, 0], in_=rows4(query))
-        nc.sync.dma_start(out=q_raw[:, 1], in_=rows4(query2))
+        for h in range(2):
+            nc.scalar.activation(out=w_dst(h), in_=w_src[:, :, :, 2 * h : 2 * h + 2], func=ACT.Copy)
+        expo = tile("expo", [P, I], F32, tag="q_raw0")
+        nc.scalar.activation(out=expo[:], in_=a[:], func=ACT.Exp, bias=neg_max[:])
+        gate = tile("gate", [P, I], F32, tag="neg_max")
+        nc.scalar.activation(out=gate[:], in_=b[:], func=ACT.Sigmoid)
         for h in range(2):
             nc.vector.quantize_mx(out=w_code[h][:].bitcast(FP8X4), scales=w_scale[h][:], in_=w_bf[h][:])
-
-        g_raw = tile("g_raw", [P, PACK, Q], F32, tag="w_bf0")
-        nc.sync.dma_start(out=g_raw[:], in_=rows4(gout))
-        nshare = tile("nshare", [P, PACK], F32)
-        nc.scalar.mul(nshare[:], share_sb[:], -1.0 / PAGE)
 
         first = CHUNK // 16
         nc.vector.tensor_copy(tab_gw[:, :CHUNK], tab_w[:].indirect(offsets[:, :first]))
         nc.vector.tensor_copy(tab_gw[:, CHUNK:], tab_w[:].indirect(offsets[:, first:]))
-
-        nc.vector.tensor_copy(key_gs[:], key_s[:].indirect(offsets[:]))
-        acc = tile("acc", [P, T], F32, tag="tab_w")
-        nc.sync.dma_start(out=acc[:], in_=old)
 
         zh = [ps.tile([P, PACK, CHUNK], F32, name="zh%d" % c) for c in range(CHUNKS)]
         for c in range(CHUNKS):
@@ -124,15 +167,8 @@ def tile_attend_blrcentred_asked_kernel(
                     stop=True,
                 )
 
-        def interleave(dst, src):
-            nc.scalar.copy(
-                out=dst.rearrange("p (c i j) -> p c j i", i=4, j=PACK),
-                in_=src.rearrange("p j (c i) -> p c j i", i=4),
-            )
-
         sums = [tile("sums%d" % c, [P, PACK, PAGES], F32) for c in range(CHUNKS)]
-        shift = [tile("shift%d" % c, [P, PAGES, PACK], F32) for c in range(CHUNKS)]
-        centred = [tile("centred%d" % c, [P, CHUNK * PACK], F32) for c in range(CHUNKS)]
+        centred = [tile("centred%d" % c, [P, PACK, CHUNK], F32) for c in range(CHUNKS)]
         hv = [tile("hv%d" % c, [P, CHUNK * PACK], F32) for c in range(CHUNKS)]
         h_bf = [tile("h_bf%d" % c, [P, CHUNK * PACK], BF16) for c in range(CHUNKS)]
         h_code = [tile("h_code%d" % c, [P, CHUNK], U32) for c in range(CHUNKS)]
@@ -147,25 +183,25 @@ def tile_attend_blrcentred_asked_kernel(
                 op=ALU.add,
             )
 
-        def page_shift(c):
-            nc.vector.tensor_tensor(
-                out=shift[c][:].rearrange("p g t -> p t g"),
-                in0=sums[c][:],
-                in1=nshare[:].unsqueeze(2).broadcast_to([P, PACK, PAGES]),
-                op=ALU.mult,
-            )
-
         def centre(c):
-            nc.vector.tensor_tensor(
-                out=centred[c][:].rearrange("p (g e t) -> p g e t", e=PAGE, t=PACK),
-                in0=zh[c][:].rearrange("p t (g e) -> p g e t", e=PAGE),
-                in1=shift[c][:].unsqueeze(2).broadcast_to([P, PAGES, PAGE, PACK]),
-                op=ALU.add,
+            for t in range(PACK):
+                nc.vector.scalar_tensor_tensor(
+                    out=centred[c][:, t, :].rearrange("p (g e) -> p g e", e=PAGE),
+                    in0=sums[c][:, t, :].unsqueeze(2).broadcast_to([P, PAGES, PAGE]),
+                    scalar=nshare[:, t : t + 1],
+                    in1=zh[c][:, t, :].rearrange("p (g e) -> p g e", e=PAGE),
+                    op0=ALU.mult,
+                    op1=ALU.add,
+                )
+            nc.scalar.activation(
+                out=hv[c][:].rearrange("p (x i t) -> p x t i", i=4, t=PACK),
+                in_=centred[c][:].rearrange("p t (x i) -> p x t i", i=4),
+                func=ACT.Tanh,
             )
-            nc.scalar.activation(out=hv[c][:], in_=centred[c][:], func=ACT.Tanh)
 
         def scale_hidden(c):
-            nc.vector.tensor_tensor(
+            engine = nc.vector if c == CHUNKS - 1 else nc.gpsimd
+            engine.tensor_tensor(
                 out=h_bf[c][:].rearrange("p (i t) -> p i t", t=PACK),
                 in0=hv[c][:].rearrange("p (i t) -> p i t", t=PACK),
                 in1=hsc_sb[:].unsqueeze(1).broadcast_to([P, CHUNK, PACK]),
@@ -188,73 +224,33 @@ def tile_attend_blrcentred_asked_kernel(
                 stop=True,
             )
 
-        q_bf = tile("q_bf", [P, 2 * Q * PACK], BF16)
-        q_code = tile("q_code", [P, 2 * Q], U32)
-        q_scale = tile("q_scale", [P, 2 * Q], U8)
-        score = [ps.tile([P, I], F32, name="score%d" % n) for n in range(2)]
-        neg_max = tile("neg_max", [P, 1], F32)
-        expo = tile("expo", [P, I], F32)
-        gate = tile("gate", [P, I], F32)
-        prob = tile("prob", [P, I], F32)
-        z = tile("z", [P, 1], F32)
-        inv_z = tile("inv_z", [P, 1], F32)
-        up = tile("up", [P, 1], F32)
-        down = tile("down", [P, 1], F32)
-        nc.vector.tensor_copy(key_gw[:], key_w[:].indirect(offsets[:]))
-        interleave(q_bf[:, : Q * PACK], q_raw[:, 0])
-        interleave(q_bf[:, Q * PACK :], q_raw[:, 1])
-        nc.vector.quantize_mx(out=q_code[:].bitcast(FP8X4), scales=q_scale[:], in_=q_bf[:])
-        for n in range(2):
-            qcols = slice(n * Q, (n + 1) * Q)
-            nc.tensor.matmul_mx(
-                out=score[n][:],
-                lhsT=q_code[:, qcols].bitcast(FP8X4),
-                lhsT_scale=q_scale[:, qcols],
-                rhs=key_gw[:].bitcast(FP8X4),
-                rhs_scale=key_gs[KEY_ROW:, :],
-                start=True,
-                stop=True,
-            )
-        nc.vector.tensor_reduce(out=neg_max[:], in_=score[0][:], axis=AXIS_X, op=ALU.max, negate=True)
-        nc.scalar.activation(out=expo[:], in_=score[0][:], func=ACT.Exp, bias=neg_max[:])
-        nc.scalar.activation(out=gate[:], in_=score[1][:], func=ACT.Sigmoid)
-        interleave(g_bf[:], g_raw[:])
+        interleave(nc.scalar.copy, g_bf[:], g_raw[:])
         page_sums(0)
         page_sums(1)
-        page_shift(0)
-        page_shift(1)
         centre(0)
-        centre(1)
-        page_sums(2)
-        page_sums(3)
-        page_shift(2)
-        page_shift(3)
-        centre(2)
-        scale_hidden(0)
-        centre(3)
-        nc.vector.quantize_mx(out=g_code[:].bitcast(FP8X4), scales=g_scale[:], in_=g_bf[:])
-        scale_hidden(1)
-        read_back(0)
+        prob = tile("prob", [P, I], F32, tag="sums0")
         nc.vector.scalar_tensor_tensor(
             out=prob[:], in0=expo[:], scalar=1.0, in1=gate[:], op0=ALU.mult, op1=ALU.mult, accum_out=z[:]
         )
-        scale_hidden(2)
-        read_back(1)
+        for c in range(1, CHUNKS):
+            if c + 1 < CHUNKS:
+                page_sums(c + 1)
+            centre(c)
         nc.vector.reciprocal(inv_z[:], z[:])
-        nc.scalar.mul(up[:], inv_z[:], 512.0)
-        nc.scalar.mul(down[:], inv_z[:], -1.0)
-        scale_hidden(3)
-        read_back(2)
-        read_back(3)
+        nc.vector.tensor_scalar(out=over_z[:], in0=factors[:], scalar1=inv_z[:], scalar2=None, op0=ALU.mult)
+        nc.vector.quantize_mx(out=g_code[:].bitcast(FP8X4), scales=g_scale[:], in_=g_bf[:])
+        for c in range(CHUNKS):
+            scale_hidden(c)
+            read_back(c)
 
         direct = tile("direct", [P, I], F32)
         total = tile("total", [P, 1], F32)
         through_z = tile("through_z", [P, I], F32)
         nc.vector.scalar_tensor_tensor(
-            out=direct[:], in0=c0[:], scalar=up[:], in1=prob[:], op0=ALU.mult, op1=ALU.mult, accum_out=total[:]
+            out=direct[:], in0=c0[:], scalar=over_z[:, 0:1], in1=prob[:], op0=ALU.mult, op1=ALU.mult, accum_out=total[:]
         )
         nc.vector.tensor_scalar(
-            out=through_z[:], in0=prob[:], scalar1=total[:], scalar2=down[:], op0=ALU.mult, op1=ALU.mult
+            out=through_z[:], in0=prob[:], scalar1=total[:], scalar2=over_z[:, 1:2], op0=ALU.mult, op1=ALU.mult
         )
         nc.vector.tensor_tensor(placed[:].indirect(offsets[:]), direct[:], through_z[:], ALU.add)
         for s in range(T // STORE):

@@ -23,7 +23,7 @@ CHUNK = 128
 CHUNKS = I // CHUNK
 PAGES = CHUNK // PAGE
 KEY_ROW = 4
-STORE = 512
+STORE_EDGES = (0, 256, 768, 1280, 1792, 2048)
 
 
 def tile_attend_blrcentred_asked_kernel(
@@ -75,6 +75,9 @@ def tile_attend_blrcentred_asked_kernel(
         nc.gpsimd.dma_start(out=share_sb[:], in_=share.rearrange("(p j) o -> p (j o)", j=PACK))
         nc.gpsimd.dma_start(out=hsc_sb[:], in_=hsc.rearrange("(p j) o -> p (j o)", j=PACK))
         nc.vector.memset(placed[:], 0.0)
+        tab_s = tile("tab_s", [P, T], U8)
+        nc.vector.memset(tab_s[:].bitcast(I32), 0)
+        load_scale_rows(nc.scalar, tab_s, tab_scales, 0)
         factors = tile("factors", [P, 2], F32)
         nc.vector.memset(factors[:, 0:1], 512.0)
         nc.vector.memset(factors[:, 1:2], -1.0)
@@ -84,7 +87,7 @@ def tile_attend_blrcentred_asked_kernel(
         )
 
         tab_gs = tile("tab_gs", [P, I], U8)
-        tab_gw = tile("tab_gw", [P, I], U32)
+        tab_gw = [tile("tab_gw_first", [P, CHUNK], U32), tile("tab_gw_rest", [P, I - CHUNK], U32)]
         key_gs = tile("key_gs", [P, I], U8)
         key_gw = tile("key_gw", [P, I], U32)
         q_bf = tile("q_bf", [P, 2 * Q * PACK], BF16)
@@ -93,15 +96,11 @@ def tile_attend_blrcentred_asked_kernel(
         neg_max = tile("neg_max", [P, 1], F32)
         z = tile("z", [P, 1], F32)
         inv_z = tile("inv_z", [P, 1], F32)
-        over_z = tile("over_z", [P, 2], F32)
 
         interleave(nc.vector.tensor_copy, q_bf[:, : Q * PACK], q_raw[0][:])
         w_raw = tile("w_raw", [P, PACK, R], F32, tag="q_raw0")
         nc.sync.dma_start(out=w_raw[:], in_=rows4(w1))
         interleave(nc.vector.tensor_copy, q_bf[:, Q * PACK :], q_raw[1][:])
-        tab_s = tile("tab_s", [P, T], U8, tag="q_raw1")
-        nc.vector.memset(tab_s[:].bitcast(I32), 0)
-        load_scale_rows(nc.scalar, tab_s, tab_scales, 0)
         nc.vector.quantize_mx(out=q_code[:].bitcast(FP8X4), scales=q_scale[:], in_=q_bf[:])
         tab_w = tile("tab_w", [P, T], U32, tag="q_bf")
         load_words(nc.sync, tab_w, tab_words)
@@ -139,8 +138,10 @@ def tile_attend_blrcentred_asked_kernel(
         def w_dst(h):
             return w_bf[h][:].rearrange("p (t m j) -> p m j t", t=2, j=PACK)
 
-        for h in range(2):
-            nc.scalar.activation(out=w_dst(h), in_=w_src[:, :, :, 2 * h : 2 * h + 2], func=ACT.Copy)
+        half = P // 2
+        nc.scalar.activation(out=w_dst(0), in_=w_src[:, :, :, 0:2], func=ACT.Copy)
+        nc.vector.tensor_copy(out=w_dst(1)[:, :half], in_=w_src[:, :half, :, 2:4])
+        nc.scalar.activation(out=w_dst(1)[:, half:], in_=w_src[:, half:, :, 2:4], func=ACT.Copy)
         expo = tile("expo", [P, I], F32, tag="q_raw0")
         nc.scalar.activation(out=expo[:], in_=a[:], func=ACT.Exp, bias=neg_max[:])
         gate = tile("gate", [P, I], F32, tag="neg_max")
@@ -149,19 +150,20 @@ def tile_attend_blrcentred_asked_kernel(
             nc.vector.quantize_mx(out=w_code[h][:].bitcast(FP8X4), scales=w_scale[h][:], in_=w_bf[h][:])
 
         first = CHUNK // 16
-        nc.vector.tensor_copy(tab_gw[:, :CHUNK], tab_w[:].indirect(offsets[:, :first]))
-        nc.vector.tensor_copy(tab_gw[:, CHUNK:], tab_w[:].indirect(offsets[:, first:]))
+        nc.vector.tensor_copy(tab_gw[0][:], tab_w[:].indirect(offsets[:, :first]))
+        nc.vector.tensor_copy(tab_gw[1][:], tab_w[:].indirect(offsets[:, first:]))
 
         zh = [ps.tile([P, PACK, CHUNK], F32, name="zh%d" % c) for c in range(CHUNKS)]
         for c in range(CHUNKS):
             cols = slice(c * CHUNK, (c + 1) * CHUNK)
+            words = tab_gw[0][:] if c == 0 else tab_gw[1][:, (c - 1) * CHUNK : c * CHUNK]
             for t in range(PACK):
                 wcols = slice((t % 2) * P, (t % 2 + 1) * P)
                 nc.tensor.matmul_mx(
                     out=zh[c][:, t, :],
                     lhsT=w_code[t // 2][:, wcols].bitcast(FP8X4),
                     lhsT_scale=w_scale[t // 2][:, wcols],
-                    rhs=tab_gw[:, cols].bitcast(FP8X4),
+                    rhs=words.bitcast(FP8X4),
                     rhs_scale=tab_gs[:, cols],
                     start=True,
                     stop=True,
@@ -170,9 +172,7 @@ def tile_attend_blrcentred_asked_kernel(
         sums = [tile("sums%d" % c, [P, PACK, PAGES], F32) for c in range(CHUNKS)]
         centred = [tile("centred%d" % c, [P, PACK, CHUNK], F32) for c in range(CHUNKS)]
         hv = [tile("hv%d" % c, [P, CHUNK * PACK], F32) for c in range(CHUNKS)]
-        h_bf = [tile("h_bf%d" % c, [P, CHUNK * PACK], BF16) for c in range(CHUNKS)]
-        h_code = [tile("h_code%d" % c, [P, CHUNK], U32) for c in range(CHUNKS)]
-        h_scale = [tile("h_scale%d" % c, [P, CHUNK], U8) for c in range(CHUNKS)]
+        gh_bf = tile("gh_bf", [P, (Q + I) * PACK], BF16)
         c0 = ps.tile([P, I], F32, name="c0")
 
         def page_sums(c):
@@ -200,48 +200,61 @@ def tile_attend_blrcentred_asked_kernel(
             )
 
         def scale_hidden(c):
-            engine = nc.vector if c == CHUNKS - 1 else nc.gpsimd
+            engine = nc.gpsimd if c < CHUNKS // 2 else nc.vector
             engine.tensor_tensor(
-                out=h_bf[c][:].rearrange("p (i t) -> p i t", t=PACK),
+                out=gh_bf[:, (Q + c * CHUNK) * PACK : (Q + (c + 1) * CHUNK) * PACK].rearrange("p (i t) -> p i t", t=PACK),
                 in0=hv[c][:].rearrange("p (i t) -> p i t", t=PACK),
                 in1=hsc_sb[:].unsqueeze(1).broadcast_to([P, CHUNK, PACK]),
                 op=ALU.mult,
             )
 
-        g_bf = tile("g_bf", [P, Q * PACK], BF16)
-        g_code = tile("g_code", [P, Q], U32)
-        g_scale = tile("g_scale", [P, Q], U8)
+        def quantize(first_col, end_col):
+            nc.vector.quantize_mx(
+                out=gh_code[:, first_col:end_col].bitcast(FP8X4),
+                scales=gh_scale[:, first_col:end_col],
+                in_=gh_bf[:, first_col * PACK : end_col * PACK],
+            )
 
-        def read_back(c):
-            nc.vector.quantize_mx(out=h_code[c][:].bitcast(FP8X4), scales=h_scale[c][:], in_=h_bf[c][:])
+        def read_back(first_slot, end_slot):
+            cols = slice(Q + first_slot, Q + end_slot)
             nc.tensor.matmul_mx(
-                out=c0[:, c * CHUNK : (c + 1) * CHUNK],
-                lhsT=g_code[:].bitcast(FP8X4),
-                lhsT_scale=g_scale[:],
-                rhs=h_code[c][:].bitcast(FP8X4),
-                rhs_scale=h_scale[c][:],
+                out=c0[:, first_slot:end_slot],
+                lhsT=gh_code[:, :Q].bitcast(FP8X4),
+                lhsT_scale=gh_scale[:, :Q],
+                rhs=gh_code[:, cols].bitcast(FP8X4),
+                rhs_scale=gh_scale[:, cols],
                 start=True,
                 stop=True,
             )
 
-        interleave(nc.scalar.copy, g_bf[:], g_raw[:])
+        gated = tile("gated", [P, I], F32)
+        prob = tile("prob", [P, I], F32)
+        nc.gpsimd.tensor_tensor(out=gated[:], in0=expo[:], in1=gate[:], op=ALU.mult)
+        interleave(nc.scalar.copy, gh_bf[:, : Q * PACK], g_raw[:])
         page_sums(0)
         page_sums(1)
         centre(0)
-        prob = tile("prob", [P, I], F32, tag="sums0")
-        nc.vector.scalar_tensor_tensor(
-            out=prob[:], in0=expo[:], scalar=1.0, in1=gate[:], op0=ALU.mult, op1=ALU.mult, accum_out=z[:]
-        )
-        for c in range(1, CHUNKS):
-            if c + 1 < CHUNKS:
-                page_sums(c + 1)
-            centre(c)
+        nc.scalar.activation(out=prob[:], in_=gated[:], func=ACT.Copy, accum_out=z[:])
+        scale_hidden(0)
+        page_sums(2)
+        centre(1)
+        scale_hidden(1)
+        page_sums(3)
+        centre(2)
+        centre(3)
+        gh_code = tile("gh_code", [P, Q + I], U32, tag="sums3")
+        gh_scale = tile("gh_scale", [P, Q + I], U8)
+        over_z = tile("over_z", [P, 2], F32, tag="nshare")
         nc.vector.reciprocal(inv_z[:], z[:])
+        scale_hidden(2)
+        quantize(0, Q + 2 * CHUNK)
+        read_back(0, 2 * CHUNK)
+        quantize(Q + 2 * CHUNK, Q + 3 * CHUNK)
+        read_back(2 * CHUNK, 3 * CHUNK)
+        scale_hidden(3)
         nc.vector.tensor_scalar(out=over_z[:], in0=factors[:], scalar1=inv_z[:], scalar2=None, op0=ALU.mult)
-        nc.vector.quantize_mx(out=g_code[:].bitcast(FP8X4), scales=g_scale[:], in_=g_bf[:])
-        for c in range(CHUNKS):
-            scale_hidden(c)
-            read_back(c)
+        quantize(Q + 3 * CHUNK, Q + I)
+        read_back(3 * CHUNK, I)
 
         direct = tile("direct", [P, I], F32)
         total = tile("total", [P, 1], F32)
@@ -253,7 +266,7 @@ def tile_attend_blrcentred_asked_kernel(
             out=through_z[:], in0=prob[:], scalar1=total[:], scalar2=over_z[:, 1:2], op0=ALU.mult, op1=ALU.mult
         )
         nc.vector.tensor_tensor(placed[:].indirect(offsets[:]), direct[:], through_z[:], ALU.add)
-        for s in range(T // STORE):
-            cols = slice(s * STORE, (s + 1) * STORE)
+        for lo, hi in zip(STORE_EDGES, STORE_EDGES[1:]):
+            cols = slice(lo, hi)
             nc.vector.tensor_tensor(out=acc[:, cols], in0=acc[:, cols], in1=placed[:, cols], op=ALU.add)
             nc.sync.dma_start(out=out[:, cols], in_=acc[:, cols])

@@ -22,7 +22,10 @@ PAGE = I // G
 CHUNK = 128
 CHUNKS = I // CHUNK
 PAGES = CHUNK // PAGE
+LIST_ROWS = 16
+LINE = 4
 KEY_ROW = 4
+GRAD_SCALE = 512.0
 STORE_EDGES = (0, 256, 768, 1280, 1792, 2048)
 
 
@@ -37,23 +40,23 @@ def tile_attend_blrcentred_asked_kernel(
         def tile(name, shape, dtype, tag=None):
             return sb.tile(shape, dtype, name=name, tag=tag or name, align_bytes=64)
 
-        offsets = sb.tile([P, I // 16], U16, name="offsets")
-        key_w = tile("key_w", [P, T], U32)
+        offsets = sb.tile([P, I // LIST_ROWS], U16, name="offsets")
+        w_raw = tile("w_raw", [P, PACK, R], F32)
         key_s = tile("key_s", [P, T], U8)
         q_raw = [tile("q_raw%d" % n, [P, PACK, Q], F32) for n in range(2)]
         share_sb = tile("share_sb", [P, PACK], F32)
         hsc_sb = tile("hsc_sb", [P, PACK], F32)
         placed = tile("placed", [P, T], F32)
 
-        def load_scale_rows(queue, plane, scales, first_row):
+        def load_scale_rows(queues, scale_tile, scales, first_row):
             for r in range(4):
-                queue.dma_start(
-                    out=plane[first_row + r : P : 32, :].bitcast(I32),
+                queues[r].dma_start(
+                    out=scale_tile[first_row + r : P : 32, :].bitcast(I32),
                     in_=scales[0, r:16:4, :].bitcast(I32),
                 )
 
-        def load_words(queue, words_sb, words):
-            queue.dma_start(
+        def load_words(words_sb, words):
+            nc.sync.dma_start(
                 out=words_sb[:].bitcast(I32), in_=words[0].rearrange("p n t -> p (n t)").bitcast(I32)
             )
 
@@ -62,31 +65,30 @@ def tile_attend_blrcentred_asked_kernel(
 
         def interleave(copy, dst, src):
             copy(
-                out=dst.rearrange("p (c i j) -> p c j i", i=4, j=PACK),
-                in_=src.rearrange("p j (c i) -> p c j i", i=4),
+                out=dst.rearrange("p (c i j) -> p c j i", i=LINE, j=PACK),
+                in_=src.rearrange("p j (c i) -> p c j i", i=LINE),
             )
 
         nc.vector.memset(key_s[:].bitcast(I32), 0)
         nc.sync.dma_start(offsets[:], offs)
         nc.sync.dma_start(out=q_raw[0][:], in_=rows4(query))
         nc.sync.dma_start(out=q_raw[1][:], in_=rows4(query2))
-        load_words(nc.sync, key_w, keys_words)
-        load_scale_rows(nc.scalar, key_s, keys_scales, KEY_ROW)
+        nc.sync.dma_start(out=w_raw[:], in_=rows4(w1))
+        load_scale_rows([nc.scalar] * 4, key_s, keys_scales, KEY_ROW)
+        tab_s = tile("tab_s", [P, T], U8)
+        nc.gpsimd.memset(tab_s[:].bitcast(I32), 0)
+        load_scale_rows([nc.scalar, nc.scalar, nc.gpsimd, nc.gpsimd], tab_s, tab_scales, 0)
         nc.gpsimd.dma_start(out=share_sb[:], in_=share.rearrange("(p j) o -> p (j o)", j=PACK))
         nc.gpsimd.dma_start(out=hsc_sb[:], in_=hsc.rearrange("(p j) o -> p (j o)", j=PACK))
         nc.vector.memset(placed[:], 0.0)
-        tab_s = tile("tab_s", [P, T], U8)
-        nc.vector.memset(tab_s[:].bitcast(I32), 0)
-        load_scale_rows(nc.scalar, tab_s, tab_scales, 0)
         factors = tile("factors", [P, 2], F32)
-        nc.vector.memset(factors[:, 0:1], 512.0)
+        nc.vector.memset(factors[:, 0:1], GRAD_SCALE)
         nc.vector.memset(factors[:, 1:2], -1.0)
         nshare = tile("nshare", [P, PACK], F32)
         nc.gpsimd.tensor_scalar(
             out=nshare[:], in0=share_sb[:], scalar1=-1.0 / PAGE, scalar2=0.0, op0=ALU.mult, op1=ALU.add
         )
 
-        tab_gs = tile("tab_gs", [P, I], U8)
         tab_gw = [tile("tab_gw_first", [P, CHUNK], U32), tile("tab_gw_rest", [P, I - CHUNK], U32)]
         key_gs = tile("key_gs", [P, I], U8)
         key_gw = tile("key_gw", [P, I], U32)
@@ -98,17 +100,19 @@ def tile_attend_blrcentred_asked_kernel(
         inv_z = tile("inv_z", [P, 1], F32)
 
         interleave(nc.vector.tensor_copy, q_bf[:, : Q * PACK], q_raw[0][:])
-        w_raw = tile("w_raw", [P, PACK, R], F32, tag="q_raw0")
-        nc.sync.dma_start(out=w_raw[:], in_=rows4(w1))
+        key_w = tile("key_w", [P, T], U32, tag="q_raw0")
+        load_words(key_w, keys_words)
         interleave(nc.vector.tensor_copy, q_bf[:, Q * PACK :], q_raw[1][:])
         nc.vector.quantize_mx(out=q_code[:].bitcast(FP8X4), scales=q_scale[:], in_=q_bf[:])
         tab_w = tile("tab_w", [P, T], U32, tag="q_bf")
-        load_words(nc.sync, tab_w, tab_words)
+        load_words(tab_w, tab_words)
         nc.vector.tensor_copy(key_gs[:], key_s[:].indirect(offsets[:]))
-        g_raw = tile("g_raw", [P, PACK, Q], F32, tag="key_s")
+        tab_gs = tile("tab_gs", [P, I], U8, tag="key_s")
+        nc.vector.tensor_copy(tab_gs[:], tab_s[:].indirect(offsets[:]))
+        g_raw = tile("g_raw", [P, PACK, Q], F32, tag="tab_s")
         nc.sync.dma_start(out=g_raw[:], in_=rows4(gout))
         nc.vector.tensor_copy(key_gw[:], key_w[:].indirect(offsets[:]))
-        acc = tile("acc", [P, T], F32, tag="key_w")
+        acc = tile("acc", [P, T], F32, tag="q_raw0")
         nc.sync.dma_start(out=acc[:], in_=old)
 
         def scores(n):
@@ -129,27 +133,25 @@ def tile_attend_blrcentred_asked_kernel(
         b = scores(1)
         nc.vector.tensor_reduce(out=neg_max[:], in_=a[:], axis=AXIS_X, op=ALU.max, negate=True)
 
-        nc.vector.tensor_copy(tab_gs[:], tab_s[:].indirect(offsets[:]))
         w_bf = [tile("w_bf%d" % h, [P, 2 * P * PACK], BF16) for h in range(2)]
         w_code = [tile("w_code%d" % h, [P, 2 * P], U32) for h in range(2)]
         w_scale = [tile("w_scale%d" % h, [P, 2 * P], U8) for h in range(2)]
         w_src = w_raw[:].rearrange("p j (m t) -> p m j t", t=PACK)
+        for h in range(2):
+            nc.scalar.activation(
+                out=w_bf[h][:].rearrange("p (t m j) -> p m j t", t=2, j=PACK),
+                in_=w_src[:, :, :, 2 * h : 2 * h + 2],
+                func=ACT.Copy,
+            )
 
-        def w_dst(h):
-            return w_bf[h][:].rearrange("p (t m j) -> p m j t", t=2, j=PACK)
-
-        half = P // 2
-        nc.scalar.activation(out=w_dst(0), in_=w_src[:, :, :, 0:2], func=ACT.Copy)
-        nc.vector.tensor_copy(out=w_dst(1)[:, :half], in_=w_src[:, :half, :, 2:4])
-        nc.scalar.activation(out=w_dst(1)[:, half:], in_=w_src[:, half:, :, 2:4], func=ACT.Copy)
-        expo = tile("expo", [P, I], F32, tag="q_raw0")
+        expo = tile("expo", [P, I], F32, tag="w_raw")
         nc.scalar.activation(out=expo[:], in_=a[:], func=ACT.Exp, bias=neg_max[:])
         gate = tile("gate", [P, I], F32, tag="neg_max")
         nc.scalar.activation(out=gate[:], in_=b[:], func=ACT.Sigmoid)
         for h in range(2):
             nc.vector.quantize_mx(out=w_code[h][:].bitcast(FP8X4), scales=w_scale[h][:], in_=w_bf[h][:])
 
-        first = CHUNK // 16
+        first = CHUNK // LIST_ROWS
         nc.vector.tensor_copy(tab_gw[0][:], tab_w[:].indirect(offsets[:, :first]))
         nc.vector.tensor_copy(tab_gw[1][:], tab_w[:].indirect(offsets[:, first:]))
 
@@ -194,8 +196,8 @@ def tile_attend_blrcentred_asked_kernel(
                     op1=ALU.add,
                 )
             nc.scalar.activation(
-                out=hv[c][:].rearrange("p (x i t) -> p x t i", i=4, t=PACK),
-                in_=centred[c][:].rearrange("p t (x i) -> p x t i", i=4),
+                out=hv[c][:].rearrange("p (x i t) -> p x t i", i=LINE, t=PACK),
+                in_=centred[c][:].rearrange("p t (x i) -> p x t i", i=LINE),
                 func=ACT.Tanh,
             )
 

from contextlib import ExitStack

import concourse.mybir as mybir

D, K, R, T, I, Q, G = 512, 512, 512, 2048, 512, 128, 32
FLOPS = 2 * (2 * D * Q * I + K * R * I + R * Q * I)

F32 = mybir.dt.float32
BF16 = mybir.dt.bfloat16
I32 = mybir.dt.int32
U32 = mybir.dt.uint32
U16 = mybir.dt.uint16
U8 = mybir.dt.uint8
FP8X4 = mybir.dt.float8_e4m3fn_x4
ALU = mybir.AluOpType
ACT = mybir.ActivationFunctionType
AXIS_X = mybir.AxisListType.X

P = 128
PACK = 4
PAGE = I // G
CHUNK = 128
CHUNKS = I // CHUNK
PAGES = CHUNK // PAGE
LIST_ROWS = 16
LINE = 4
KEY_ROW = 4
GRAD_SCALE = 512.0
STORE_EDGES = (0, 256, 768, 1280, 1792, 2048)


def tile_attend_blrcentred_asked_kernel(
    tc, query, query2, keys_words, keys_scales, tab_words, tab_scales, w1, share, gout, hsc, old, offs, out
):
    nc = tc.nc
    with ExitStack() as ctx:
        sb = ctx.enter_context(tc.tile_pool(name="sb", bufs=1))
        ps = ctx.enter_context(tc.psum_pool(name="ps", bufs=1))

        def tile(name, shape, dtype, tag=None):
            return sb.tile(shape, dtype, name=name, tag=tag or name, align_bytes=64)

        offsets = sb.tile([P, I // LIST_ROWS], U16, name="offsets")
        w_raw = tile("w_raw", [P, PACK, R], F32)
        key_s = tile("key_s", [P, T], U8)
        q_raw = [tile("q_raw%d" % n, [P, PACK, Q], F32) for n in range(2)]
        share_sb = tile("share_sb", [P, PACK], F32)
        hsc_sb = tile("hsc_sb", [P, PACK], F32)
        placed = tile("placed", [P, T], F32)

        def load_scale_rows(queues, scale_tile, scales, first_row):
            for r in range(4):
                queues[r].dma_start(
                    out=scale_tile[first_row + r : P : 32, :].bitcast(I32),
                    in_=scales[0, r:16:4, :].bitcast(I32),
                )

        def load_words(words_sb, words):
            nc.sync.dma_start(
                out=words_sb[:].bitcast(I32), in_=words[0].rearrange("p n t -> p (n t)").bitcast(I32)
            )

        def rows4(ap):
            return ap.rearrange("(p j) c -> p j c", j=PACK)

        def interleave(copy, dst, src):
            copy(
                out=dst.rearrange("p (c i j) -> p c j i", i=LINE, j=PACK),
                in_=src.rearrange("p j (c i) -> p c j i", i=LINE),
            )

        nc.vector.memset(key_s[:].bitcast(I32), 0)
        nc.sync.dma_start(offsets[:], offs)
        nc.sync.dma_start(out=q_raw[0][:], in_=rows4(query))
        nc.sync.dma_start(out=q_raw[1][:], in_=rows4(query2))
        nc.sync.dma_start(out=w_raw[:], in_=rows4(w1))
        load_scale_rows([nc.scalar] * 4, key_s, keys_scales, KEY_ROW)
        tab_s = tile("tab_s", [P, T], U8)
        nc.gpsimd.memset(tab_s[:].bitcast(I32), 0)
        load_scale_rows([nc.scalar, nc.scalar, nc.gpsimd, nc.gpsimd], tab_s, tab_scales, 0)
        nc.gpsimd.dma_start(out=share_sb[:], in_=share.rearrange("(p j) o -> p (j o)", j=PACK))
        nc.gpsimd.dma_start(out=hsc_sb[:], in_=hsc.rearrange("(p j) o -> p (j o)", j=PACK))
        nc.vector.memset(placed[:], 0.0)
        factors = tile("factors", [P, 2], F32)
        nc.vector.memset(factors[:, 0:1], GRAD_SCALE)
        nc.vector.memset(factors[:, 1:2], -1.0)
        nshare = tile("nshare", [P, PACK], F32)
        nc.gpsimd.tensor_scalar(
            out=nshare[:], in0=share_sb[:], scalar1=-1.0 / PAGE, scalar2=0.0, op0=ALU.mult, op1=ALU.add
        )

        tab_gw = [tile("tab_gw_first", [P, CHUNK], U32), tile("tab_gw_rest", [P, I - CHUNK], U32)]
        key_gs = tile("key_gs", [P, I], U8)
        key_gw = tile("key_gw", [P, I], U32)
        q_bf = tile("q_bf", [P, 2 * Q * PACK], BF16)
        q_code = tile("q_code", [P, 2 * Q], U32)
        q_scale = tile("q_scale", [P, 2 * Q], U8)
        neg_max = tile("neg_max", [P, 1], F32)
        z = tile("z", [P, 1], F32)
        inv_z = tile("inv_z", [P, 1], F32)

        interleave(nc.vector.tensor_copy, q_bf[:, : Q * PACK], q_raw[0][:])
        key_w = tile("key_w", [P, T], U32, tag="q_raw0")
        load_words(key_w, keys_words)
        interleave(nc.vector.tensor_copy, q_bf[:, Q * PACK :], q_raw[1][:])
        nc.vector.quantize_mx(out=q_code[:].bitcast(FP8X4), scales=q_scale[:], in_=q_bf[:])
        tab_w = tile("tab_w", [P, T], U32, tag="q_bf")
        load_words(tab_w, tab_words)
        nc.vector.tensor_copy(key_gs[:], key_s[:].indirect(offsets[:]))
        tab_gs = tile("tab_gs", [P, I], U8, tag="key_s")
        nc.vector.tensor_copy(tab_gs[:], tab_s[:].indirect(offsets[:]))
        g_raw = tile("g_raw", [P, PACK, Q], F32, tag="tab_s")
        nc.sync.dma_start(out=g_raw[:], in_=rows4(gout))
        nc.vector.tensor_copy(key_gw[:], key_w[:].indirect(offsets[:]))
        acc = tile("acc", [P, T], F32, tag="q_raw0")
        nc.sync.dma_start(out=acc[:], in_=old)

        def scores(n):
            bank = ps.tile([P, I], F32, name="score%d" % n)
            qcols = slice(n * Q, (n + 1) * Q)
            nc.tensor.matmul_mx(
                out=bank[:],
                lhsT=q_code[:, qcols].bitcast(FP8X4),
                lhsT_scale=q_scale[:, qcols],
                rhs=key_gw[:].bitcast(FP8X4),
                rhs_scale=key_gs[KEY_ROW:, :],
                start=True,
                stop=True,
            )
            return bank

        a = scores(0)
        b = scores(1)
        nc.vector.tensor_reduce(out=neg_max[:], in_=a[:], axis=AXIS_X, op=ALU.max, negate=True)

        w_bf = [tile("w_bf%d" % h, [P, 2 * P * PACK], BF16) for h in range(2)]
        w_code = [tile("w_code%d" % h, [P, 2 * P], U32) for h in range(2)]
        w_scale = [tile("w_scale%d" % h, [P, 2 * P], U8) for h in range(2)]
        w_src = w_raw[:].rearrange("p j (m t) -> p m j t", t=PACK)
        for h in range(2):
            nc.scalar.activation(
                out=w_bf[h][:].rearrange("p (t m j) -> p m j t", t=2, j=PACK),
                in_=w_src[:, :, :, 2 * h : 2 * h + 2],
                func=ACT.Copy,
            )

        expo = tile("expo", [P, I], F32, tag="w_raw")
        nc.scalar.activation(out=expo[:], in_=a[:], func=ACT.Exp, bias=neg_max[:])
        gate = tile("gate", [P, I], F32, tag="neg_max")
        nc.scalar.activation(out=gate[:], in_=b[:], func=ACT.Sigmoid)
        for h in range(2):
            nc.vector.quantize_mx(out=w_code[h][:].bitcast(FP8X4), scales=w_scale[h][:], in_=w_bf[h][:])

        first = CHUNK // LIST_ROWS
        nc.vector.tensor_copy(tab_gw[0][:], tab_w[:].indirect(offsets[:, :first]))
        nc.vector.tensor_copy(tab_gw[1][:], tab_w[:].indirect(offsets[:, first:]))

        zh = [ps.tile([P, PACK, CHUNK], F32, name="zh%d" % c) for c in range(CHUNKS)]
        for c in range(CHUNKS):
            cols = slice(c * CHUNK, (c + 1) * CHUNK)
            words = tab_gw[0][:] if c == 0 else tab_gw[1][:, (c - 1) * CHUNK : c * CHUNK]
            for t in range(PACK):
                wcols = slice((t % 2) * P, (t % 2 + 1) * P)
                nc.tensor.matmul_mx(
                    out=zh[c][:, t, :],
                    lhsT=w_code[t // 2][:, wcols].bitcast(FP8X4),
                    lhsT_scale=w_scale[t // 2][:, wcols],
                    rhs=words.bitcast(FP8X4),
                    rhs_scale=tab_gs[:, cols],
                    start=True,
                    stop=True,
                )

        sums = [tile("sums%d" % c, [P, PACK, PAGES], F32) for c in range(CHUNKS)]
        centred = [tile("centred%d" % c, [P, PACK, CHUNK], F32) for c in range(CHUNKS)]
        hv = [tile("hv%d" % c, [P, CHUNK * PACK], F32) for c in range(CHUNKS)]
        gh_bf = tile("gh_bf", [P, (Q + I) * PACK], BF16)
        c0 = ps.tile([P, I], F32, name="c0")

        def page_sums(c):
            nc.vector.tensor_reduce(
                out=sums[c][:].rearrange("p t g -> p (t g)"),
                in_=zh[c][:].rearrange("p t (g e) -> p (t g) e", e=PAGE),
                axis=AXIS_X,
                op=ALU.add,
            )

        def centre(c):
            for t in range(PACK):
                nc.vector.scalar_tensor_tensor(
                    out=centred[c][:, t, :].rearrange("p (g e) -> p g e", e=PAGE),
                    in0=sums[c][:, t, :].unsqueeze(2).broadcast_to([P, PAGES, PAGE]),
                    scalar=nshare[:, t : t + 1],
                    in1=zh[c][:, t, :].rearrange("p (g e) -> p g e", e=PAGE),
                    op0=ALU.mult,
                    op1=ALU.add,
                )
            nc.scalar.activation(
                out=hv[c][:].rearrange("p (x i t) -> p x t i", i=LINE, t=PACK),
                in_=centred[c][:].rearrange("p t (x i) -> p x t i", i=LINE),
                func=ACT.Tanh,
            )

        def scale_hidden(c):
            engine = nc.gpsimd if c < CHUNKS // 2 else nc.vector
            engine.tensor_tensor(
                out=gh_bf[:, (Q + c * CHUNK) * PACK : (Q + (c + 1) * CHUNK) * PACK].rearrange("p (i t) -> p i t", t=PACK),
                in0=hv[c][:].rearrange("p (i t) -> p i t", t=PACK),
                in1=hsc_sb[:].unsqueeze(1).broadcast_to([P, CHUNK, PACK]),
                op=ALU.mult,
            )

        def quantize(first_col, end_col):
            nc.vector.quantize_mx(
                out=gh_code[:, first_col:end_col].bitcast(FP8X4),
                scales=gh_scale[:, first_col:end_col],
                in_=gh_bf[:, first_col * PACK : end_col * PACK],
            )

        def read_back(first_slot, end_slot):
            cols = slice(Q + first_slot, Q + end_slot)
            nc.tensor.matmul_mx(
                out=c0[:, first_slot:end_slot],
                lhsT=gh_code[:, :Q].bitcast(FP8X4),
                lhsT_scale=gh_scale[:, :Q],
                rhs=gh_code[:, cols].bitcast(FP8X4),
                rhs_scale=gh_scale[:, cols],
                start=True,
                stop=True,
            )

        gated = tile("gated", [P, I], F32)
        prob = tile("prob", [P, I], F32)
        nc.gpsimd.tensor_tensor(out=gated[:], in0=expo[:], in1=gate[:], op=ALU.mult)
        interleave(nc.scalar.copy, gh_bf[:, : Q * PACK], g_raw[:])
        page_sums(0)
        page_sums(1)
        centre(0)
        nc.scalar.activation(out=prob[:], in_=gated[:], func=ACT.Copy, accum_out=z[:])
        scale_hidden(0)
        page_sums(2)
        centre(1)
        scale_hidden(1)
        page_sums(3)
        centre(2)
        centre(3)
        gh_code = tile("gh_code", [P, Q + I], U32, tag="sums3")
        gh_scale = tile("gh_scale", [P, Q + I], U8)
        over_z = tile("over_z", [P, 2], F32, tag="nshare")
        nc.vector.reciprocal(inv_z[:], z[:])
        scale_hidden(2)
        quantize(0, Q + 2 * CHUNK)
        read_back(0, 2 * CHUNK)
        quantize(Q + 2 * CHUNK, Q + 3 * CHUNK)
        read_back(2 * CHUNK, 3 * CHUNK)
        scale_hidden(3)
        nc.vector.tensor_scalar(out=over_z[:], in0=factors[:], scalar1=inv_z[:], scalar2=None, op0=ALU.mult)
        quantize(Q + 3 * CHUNK, Q + I)
        read_back(3 * CHUNK, I)

        direct = tile("direct", [P, I], F32)
        total = tile("total", [P, 1], F32)
        through_z = tile("through_z", [P, I], F32)
        nc.vector.scalar_tensor_tensor(
            out=direct[:], in0=c0[:], scalar=over_z[:, 0:1], in1=prob[:], op0=ALU.mult, op1=ALU.mult, accum_out=total[:]
        )
        nc.vector.tensor_scalar(
            out=through_z[:], in0=prob[:], scalar1=total[:], scalar2=over_z[:, 1:2], op0=ALU.mult, op1=ALU.mult
        )
        nc.vector.tensor_tensor(placed[:].indirect(offsets[:]), direct[:], through_z[:], ALU.add)
        for lo, hi in zip(STORE_EDGES, STORE_EDGES[1:]):
            cols = slice(lo, hi)
            nc.vector.tensor_tensor(out=acc[:, cols], in0=acc[:, cols], in1=placed[:, cols], op=ALU.add)
            nc.sync.dma_start(out=out[:, cols], in_=acc[:, cols])
